import numpy as np
import ml_dtypes


def mxq(x, axis, fmt="e4m3"):
    dtype, down = {"e4m3": (ml_dtypes.float8_e4m3fn, 7), "e5m2": (ml_dtypes.float8_e5m2, 14)}[fmt]
    v = np.moveaxis(np.asarray(x, np.float32).astype(ml_dtypes.bfloat16).astype(np.float64), axis, -1)
    blocks = v.reshape(v.shape[:-1] + (-1, 32))
    amax = np.abs(blocks).max(-1, keepdims=True)
    byte = np.maximum(np.where(amax > 0, np.frexp(amax)[1] - 1 + 127, 0) - down, 1)
    scale = np.exp2(byte - 127.0)
    codes = (blocks / scale).astype(np.float32).astype(dtype).astype(np.float64)
    return np.moveaxis((codes * scale).reshape(v.shape), -1, axis)


WIDE = False


def mx_kscale(k):
    if not WIDE:
        return np.ones(k)
    levels = np.array([10, -10, 5, -5, 0])
    if k % 512:
        return np.exp2(np.random.permutation(np.resize(levels, k // 32))).repeat(32)
    a = np.empty((k // 512, 16))
    for p in range(k // 512):
        a[p, :8] = np.random.permutation(np.resize(levels, 8))
        for g in range(8):
            far = levels[np.abs(levels - a[p, g]) >= 10]
            a[p, g + 8] = far[np.random.randint(len(far))]
    return np.exp2(a.ravel()).repeat(32)


def f64(x):
    return np.asarray(x).astype(np.float64)


def striped(idx):
    return np.tile(idx.reshape(-1, 16).T, (8, 1)).astype(np.uint16)


def unstriped(offs):
    return offs[:16].T.reshape(-1).astype(np.int64)


E2M1 = np.array([0.0, 0.5, 1.0, 1.5, 2.0, 3.0, 4.0, 6.0, -0.0, -0.5, -1.0, -1.5, -2.0, -3.0, -4.0, -6.0])


def pack_weight(w, fmt):
    k, n = w.shape
    w = f64(np.asarray(w, np.float32).astype(ml_dtypes.bfloat16)).reshape(k // 32, 32, n)
    amax = np.abs(w).max(1)
    if fmt == "e4m3":
        byte = np.frexp(amax)[1] - 1 + 127 - 7
    else:
        mant, ex = np.frexp(amax / 6.0)
        byte = np.where(mant > 0.5, ex, ex - 1) + 127
    byte = np.clip(np.where(amax > 0, byte, 1), 1, 254)
    scaled = (w * np.exp2(127.0 - byte)[:, None, :]).reshape(k, n).astype(np.float32)
    by_word = np.ascontiguousarray(scaled.reshape(k // 512, 128, 4, n).transpose(0, 1, 3, 2))
    if fmt == "e4m3":
        words = by_word.astype(ml_dtypes.float8_e4m3fn).view(np.uint8)
    else:
        c = by_word.astype(ml_dtypes.float4_e2m1fn).view(np.uint8) & 0xF
        words = (c[..., 0::2] | (c[..., 1::2] << 4)).reshape(k // 512, 128, 2 * n)
    return np.ascontiguousarray(words), np.ascontiguousarray(byte.astype(np.uint8).reshape(k // 512, 16, n))


def unpack_weight(words, scales, fmt):
    g, _, n = scales.shape
    words = np.ascontiguousarray(words).reshape(g, 128, n, -1)
    if fmt == "e4m3":
        vals = words.view(ml_dtypes.float8_e4m3fn).astype(np.float64)
    else:
        nib = np.empty((g, 128, n, 4), np.uint8)
        nib[..., 0::2] = words & 0xF
        nib[..., 1::2] = words >> 4
        vals = E2M1[nib]
    vals = vals * np.repeat(np.exp2(scales.astype(np.float64) - 127.0), 8, axis=1)[..., None]
    return vals.transpose(0, 1, 3, 2).reshape(g * 512, n)


def gelu(v):
    return 0.5 * v * (1.0 + np.tanh(np.sqrt(2.0 / np.pi) * (v + 0.044715 * v**3)))


K, H, T, S, T2, S2, T3, P = 1024, 1024, 2048, 512, 1024, 512, 2048, 512

def setup_inputs():
    n = np.random.standard_normal
    s = mx_kscale(K)[:, None]
    u = mx_kscale(H)[:, None]
    tab_words, tab_scales = pack_weight(n((K, T)) * s, "e4m3")
    tab2_words, tab2_scales = pack_weight(0.7 * n((H, T3)) / np.sqrt(H) / u, "e4m3")
    w1_words, w1_scales = pack_weight(1.5 * n((K, H)) / np.sqrt(K) / s, "e2m1")
    w3_words, w3_scales = pack_weight(0.7 * n((H, S2)) / np.sqrt(H) / u, "e2m1")
    return {"tab_words": tab_words, "tab_scales": tab_scales, "offs": striped(np.random.permutation(T)[:S]),
            "tab2_words": tab2_words, "tab2_scales": tab2_scales, "offs2": striped(np.random.permutation(T3)[:S2]),
            "offs3": striped(np.random.permutation(T2)[:S]),
            "pos1": striped(np.random.permutation(T2)[:P]), "pos2": striped(np.random.permutation(T2)[:P]),
            "w1_words": w1_words, "w1_scales": w1_scales, "w3_words": w3_words, "w3_scales": w3_scales,
            "w2": (n((K, H)) / np.sqrt(K) / s * u.T).astype(np.float32),
            "gain": (np.exp(0.3 * n(H)) * u[:, 0]).astype(np.float32),
            "wgs": np.exp(0.3 * n((128, S))).astype(np.float32),
            "page0": (n((H, T2)) * u).astype(np.float32), "base": (n((H, T2)) * u).astype(np.float32),
            "road": (0.8 * n(S2)).astype(np.float32)}

def reference(tab_words, tab_scales, offs, tab2_words, tab2_scales, offs2, offs3, pos1, pos2,
              w1_words, w1_scales, w3_words, w3_scales, w2, gain, wgs, page0, base, road):
    v = unpack_weight(tab_words, tab_scales, "e4m3")[:, unstriped(offs)]
    v2 = unpack_weight(tab2_words, tab2_scales, "e4m3")[:, unstriped(offs2)]
    x = unpack_weight(w1_words, w1_scales, "e2m1").T @ v
    bent = 0.5 * x * (1.0 + np.tanh(np.sqrt(2.0 / np.pi) * (x + 0.044715 * x ** 3)))
    h = f64(gain)[:, None] * bent + (mxq(f64(w2), 0, "e4m3").T @ v)
    page = f64(page0).copy()
    page[:, unstriped(offs3)] = np.tile(f64(wgs), (H // 128, 1)) * h
    top = np.maximum(page, f64(base))
    pageq = mxq(page, 0, "e4m3")
    topq = mxq(top, 0, "e4m3")
    e = v2.T @ pageq + unpack_weight(w3_words, w3_scales, "e2m1").T @ topq
    return (e[:, unstriped(pos1)] - f64(road)[:, None]) * e[:, unstriped(pos2)]

@@ -1,0 +1,277 @@
+from contextlib import ExitStack
+
+import concourse.mybir as mybir
+
+K, H, T, S, T2, S2, T3, NP = 1024, 1024, 2048, 512, 1024, 512, 2048, 512
+FLOPS = 2 * (2 * K * H * S + 2 * H * S2 * T2)
+
+F32 = mybir.dt.float32
+BF16 = mybir.dt.bfloat16
+I32 = mybir.dt.int32
+U32 = mybir.dt.uint32
+U16 = mybir.dt.uint16
+U8 = mybir.dt.uint8
+E4M3 = mybir.dt.float8_e4m3fn_x4
+E2M1 = mybir.dt.float4_e2m1fn_x4
+ALU = mybir.AluOpType
+ACT = mybir.ActivationFunctionType
+
+P = 128
+PACK = 4
+PASS = P * PACK
+BANK = 512
+QUADS = 4
+
+
+def tile_list_road_segment_linking_kernel(
+    tc, tab_words, tab_scales, offs, tab2_words, tab2_scales, offs2, offs3, pos1, pos2,
+    w1_words, w1_scales, w3_words, w3_scales, w2, gain, wgs, page0, base, road, out,
+):
+    nc = tc.nc
+    with ExitStack() as ctx:
+        lists = ctx.enter_context(tc.tile_pool(name="lists", bufs=1))
+        keep = ctx.enter_context(tc.tile_pool(name="keep", bufs=1))
+        ring = ctx.enter_context(tc.tile_pool(name="ring", bufs=2))
+        psum = ctx.enter_context(tc.psum_pool(name="psum", bufs=1))
+
+        def load_list(src, name):
+            dst = lists.tile([P, S // 16], U16, name=name)
+            nc.sync.dma_start(dst[:], src)
+            return dst
+
+        def zeroed_plane(width, name):
+            plane = keep.tile([P, width], U8, name=name, align_bytes=64)
+            nc.vector.memset(plane[:].bitcast(I32), 0)
+            return plane
+
+        def load_scales_side_by_side(plane, src):
+            for q in range(QUADS):
+                nc.sync.dma_start(
+                    plane[32 * q : 32 * q + 4, :].bitcast(I32).rearrange("r (a n) -> r a n", a=2),
+                    src[:, 4 * q : 4 * q + 4, :].bitcast(I32).rearrange("a r n -> r a n"),
+                )
+
+        def load_table_words(src, name):
+            words = keep.tile([P, T], U32, name=name, align_bytes=64)
+            nc.sync.dma_start(words[:].bitcast(I32), src.rearrange("p n i -> p (n i)").bitcast(I32))
+            return words
+
+        def load_fp4_words(src, cols, name):
+            words = keep.tile([P, 2 * 2 * cols], U8, name=name, align_bytes=64)
+            nc.sync.dma_start(
+                words[:].bitcast(I32).rearrange("p (a n) -> p a n", a=2),
+                src.bitcast(I32).rearrange("a p n -> p a n"),
+            )
+            return words
+
+        def load_rows(src, a, h, tag, name):
+            dst = ring.tile([P, PACK, BANK], F32, name=name, tag=tag, bufs=4)
+            rows = src[PASS * a : PASS * (a + 1), BANK * h : BANK * (h + 1)]
+            nc.sync.dma_start(dst[:], rows.rearrange("(p i) c -> p i c", i=PACK))
+            return dst
+
+        def load_page(a, t):
+            dst = keep.tile([P, T2], F32, name="page%d%d" % (a, t))
+            rows = page0[PASS * a : PASS * (a + 1), :].rearrange("(p i) n -> p i n", i=PACK)
+            nc.sync.dma_start(dst[:], rows[:, t, :])
+            return dst
+
+        w1_plane = zeroed_plane(2 * H, "w1_plane")
+        tab_plane = zeroed_plane(2 * T, "tab_plane")
+        tab2_plane = zeroed_plane(T3, "tab2_plane")
+        w3_plane = zeroed_plane(2 * S2, "w3_plane")
+
+        w2_raw, page, base_rows = {}, {}, {}
+        w1_raw = load_fp4_words(w1_words, H, "w1_raw")
+        load_scales_side_by_side(w1_plane, w1_scales)
+        tab_sb = [load_table_words(tab_words[0], "tab0")]
+        idx = load_list(offs, "idx")
+        tab_sb.append(load_table_words(tab_words[1], "tab1"))
+        load_scales_side_by_side(tab_plane, tab_scales)
+        w2_raw[0, 0] = load_rows(w2, 0, 0, "slab", "w2_raw00")
+        w2_raw[1, 0] = load_rows(w2, 1, 0, "slab", "w2_raw10")
+        idx2 = load_list(offs2, "idx2")
+        for q in range(QUADS):
+            nc.sync.dma_start(
+                tab2_plane[32 * q : 32 * q + 8, :].bitcast(I32),
+                tab2_scales[:, 4 * q : 4 * q + 4, :].bitcast(I32),
+            )
+        gain_sb = keep.tile([P, 2, PACK], F32, name="gain_sb")
+        nc.sync.dma_start(gain_sb[:], gain.rearrange("(a p t) -> p a t", a=2, t=PACK))
+        idx3 = load_list(offs3, "idx3")
+        wgs_sb = keep.tile([P, PACK * S], F32, name="wgs_sb")
+        for q in range(QUADS):
+            nc.sync.dma_start(wgs_sb[32 * q : 32 * (q + 1), :], wgs.rearrange("(p t) j -> p (t j)", t=PACK))
+        page[0, 0] = load_page(0, 0)
+        page[0, 1] = load_page(0, 1)
+        w2_raw[0, 1] = load_rows(w2, 0, 1, "slab", "w2_raw01")
+        page[0, 2] = load_page(0, 2)
+        w2_raw[1, 1] = load_rows(w2, 1, 1, "slab", "w2_raw11")
+        for t in range(PACK - 1):
+            page[1, t] = load_page(1, t)
+        page[0, 3] = load_page(0, 3)
+        page[1, 3] = load_page(1, 3)
+        for h in range(2):
+            base_rows[0, h] = load_rows(base, 0, h, "given", "base0%d" % h)
+        tab2_sb = [load_table_words(tab2_words[a], "tab2_%d" % a) for a in range(2)]
+        w3_sb = load_fp4_words(w3_words, S2, "w3_sb")
+        load_scales_side_by_side(w3_plane, w3_scales)
+        for h in range(2):
+            base_rows[1, h] = load_rows(base, 1, h, "given", "base1%d" % h)
+        p1 = load_list(pos1, "p1")
+        p2 = load_list(pos2, "p2")
+        road_sb = keep.tile([P, S2 // P], F32, name="road_sb")
+        with nc.allow_non_contiguous_dma(reason="one value of road a partition and row tile"):
+            nc.sync.dma_start(road_sb[:], road.rearrange("(m p) -> p m", p=P))
+
+        def gather(window, offsets, dtype, name):
+            dst = keep.tile([P, S], dtype, name=name, align_bytes=64)
+            nc.vector.tensor_copy(dst[:], window.indirect(offsets[:]))
+            return dst
+
+        def quantize(grouped, name):
+            codes = keep.tile([P, BANK], U32, name=name + "_codes", align_bytes=64)
+            plane = keep.tile([P, BANK], U8, name=name + "_plane", align_bytes=64)
+            nc.vector.quantize_mx(out=codes[:].bitcast(E4M3), scales=plane[:], in_=grouped[:])
+            return codes, plane
+
+        def quantize_w2(kp, a, copy):
+            grouped = ring.tile([P, PACK * BANK], BF16, name="w2_grouped", tag="grouped", align_bytes=64)
+            copy(
+                grouped[:].rearrange("p (t m i) -> p m i t", t=PACK, i=PACK),
+                w2_raw[kp, a][:].rearrange("p i (m t) -> p m i t", t=PACK),
+            )
+            return quantize(grouped, "w2_%d%d" % (kp, a))
+
+        w1_dealt = keep.tile([P, 2 * 2 * H], U8, name="w1_dealt", align_bytes=64)
+        w1_plane_dealt = keep.tile([P, 2 * H], U8, name="w1_plane_dealt", align_bytes=64)
+
+        def deal_w1(a):
+            for dst, src in ((w1_dealt[:].bitcast(U16), w1_raw[:].bitcast(U16)), (w1_plane_dealt[:], w1_plane[:])):
+                nc.vector.tensor_copy(
+                    dst.rearrange("p (k a t m) -> p a k m t", k=2, a=2, t=PACK)[:, a],
+                    src.rearrange("p (k a m t) -> p a k m t", k=2, a=2, t=PACK)[:, a],
+                )
+
+        deal_w1(0)
+        deal_w1(1)
+        v_plane = [gather(tab_plane[:, T * kp : T * (kp + 1)], idx, U8, "v_plane%d" % kp) for kp in range(2)]
+        v = [gather(tab_sb[kp][:], idx, U32, "v%d" % kp) for kp in range(2)]
+        w2_q = {(0, 0): quantize_w2(0, 0, nc.scalar.copy), (1, 0): quantize_w2(1, 0, nc.vector.tensor_copy)}
+        v2_planes = gather(tab2_plane[:], idx2, U8, "v2_planes")
+
+        def bank(i, name):
+            return psum.tile([P, BANK], F32, name=name, tag="bank%d" % (i % 8))
+
+        staged = {
+            (a, h): ring.tile([P, PACK, BANK], F32, name="staged%d%d" % (a, h), tag="slab", bufs=4)
+            for a in (1, 0) for h in range(2)
+        }
+
+        def change_page(a, t):
+            x = bank(2 * (PACK * a + t), "x")
+            y = bank(2 * (PACK * a + t) + 1, "y")
+            for kp in range(2):
+                col = H * kp + PASS * a + P * t
+                nc.tensor.matmul_mx(
+                    out=x[:], lhsT=w1_dealt[:, 2 * col : 2 * (col + P)].bitcast(E2M1),
+                    lhsT_scale=w1_plane_dealt[:, col : col + P],
+                    rhs=v[kp][:].bitcast(E4M3), rhs_scale=v_plane[kp][:], start=(kp == 0), stop=(kp == 1),
+                )
+            for kp in range(2):
+                codes, plane = w2_q[kp, a]
+                nc.tensor.matmul_mx(
+                    out=y[:], lhsT=codes[:, P * t : P * (t + 1)].bitcast(E4M3),
+                    lhsT_scale=plane[:, P * t : P * (t + 1)],
+                    rhs=v[kp][:].bitcast(E4M3), rhs_scale=v_plane[kp][:], start=(kp == 0), stop=(kp == 1),
+                )
+            bent = ring.tile([P, S], F32, name="bent", tag="first")
+            nc.scalar.activation(bent[:], x[:], ACT.Gelu_apprx_tanh)
+            feat = ring.tile([P, S], F32, name="feat", tag="second", bufs=3)
+            nc.vector.scalar_tensor_tensor(feat[:], bent[:], gain_sb[:, a, t : t + 1], y[:], ALU.mult, ALU.add)
+            nc.vector.tensor_tensor(
+                page[a, t][:].indirect(idx3[:]), feat[:], wgs_sb[:, S * t : S * (t + 1)], ALU.mult
+            )
+
+        def stage_page(a, t):
+            for h in range(2):
+                nc.scalar.copy(staged[a, h][:, t, :], page[a, t][:, BANK * h : BANK * (h + 1)])
+
+        def by_lines(rows):
+            return rows[:].rearrange("p t (c i) -> p c t i", i=4)
+
+        def grouped_by_lines(grouped):
+            return grouped[:].rearrange("p (c i t) -> p c t i", i=4, t=PACK)
+
+        page_q, top_q = {}, {}
+
+        def quantize_page(a, h):
+            page_grouped = ring.tile([P, PACK * BANK], BF16, name="page_grouped", tag="grouped", align_bytes=64)
+            nc.scalar.copy(grouped_by_lines(page_grouped), by_lines(staged[a, h]))
+            top_grouped = ring.tile([P, PACK * BANK], BF16, name="top_grouped", align_bytes=64)
+            nc.vector.tensor_tensor(
+                grouped_by_lines(top_grouped), by_lines(staged[a, h]), by_lines(base_rows[a, h]), ALU.max
+            )
+            page_q[a, h] = quantize(page_grouped, "page_%d%d" % (a, h))
+            top_q[a, h] = quantize(top_grouped, "top_%d%d" % (a, h))
+
+        for t in range(PACK - 1):
+            change_page(0, t)
+        w2_q.update({(kp, 1): quantize_w2(kp, 1, nc.scalar.copy) for kp in range(2)})
+        change_page(0, PACK - 1)
+        for t in range(PACK):
+            change_page(1, t)
+        for a in range(2):
+            for t in range(PACK):
+                stage_page(a, t)
+        for h in range(2):
+            quantize_page(0, h)
+        v2 = [gather(tab2_sb[a][:], idx2, U32, "v2_%d" % a) for a in range(2)]
+        minus_road = keep.tile([P, S2 // P], F32, name="minus_road")
+        nc.scalar.mul(minus_road[:], road_sb[:], -1.0)
+
+        score = {(m, h): bank(2 * m + h, "score%d%d" % (m, h)) for m in range(S2 // P) for h in range(2)}
+
+        def score_passes(a, h):
+            for m in range(S2 // P):
+                codes, plane = page_q[a, h]
+                nc.tensor.matmul_mx(
+                    out=score[m, h][:], lhsT=v2[a][:, P * m : P * (m + 1)].bitcast(E4M3),
+                    lhsT_scale=v2_planes[4 * a :, P * m : P * (m + 1)],
+                    rhs=codes[:].bitcast(E4M3), rhs_scale=plane[:], start=(a == 0), stop=False,
+                )
+                codes, plane = top_q[a, h]
+                col = S2 * a + P * m
+                nc.tensor.matmul_mx(
+                    out=score[m, h][:], lhsT=w3_sb[:, 2 * col : 2 * (col + P)].bitcast(E2M1),
+                    lhsT_scale=w3_plane[:, col : col + P],
+                    rhs=codes[:].bitcast(E4M3), rhs_scale=plane[:], start=False, stop=(a == 1),
+                )
+
+        for h in range(2):
+            score_passes(0, h)
+        for h in range(2):
+            quantize_page(1, h)
+            score_passes(1, h)
+
+        scores, shifted = {}, {}
+
+        def pick_first(m):
+            scores[m] = ring.tile([P, T2], F32, name="scores%d" % m, tag="given", bufs=4)
+            for h in range(2):
+                nc.scalar.copy(scores[m][:, BANK * h : BANK * (h + 1)], score[m, h][:])
+            picked = ring.tile([P, NP], F32, name="picked", tag="first")
+            nc.vector.tensor_copy(picked[:], scores[m][:].indirect(p1[:]))
+            shifted[m] = ring.tile([P, NP], F32, name="shifted", tag="second", bufs=3)
+            nc.scalar.activation(shifted[m][:], picked[:], ACT.Identity, bias=minus_road[:, m : m + 1])
+
+        def pick_second(m):
+            result = ring.tile([P, NP], F32, name="result")
+            nc.vector.tensor_tensor(result[:], scores[m][:].indirect(p2[:]), shifted[m][:], ALU.mult)
+            nc.sync.dma_start(out[P * m : P * (m + 1), :], result[:])
+
+        pick_first(0)
+        for m in range(S2 // P):
+            if m + 1 < S2 // P:
+                pick_first(m + 1)
+            pick_second(m)

@@ -84,25 +84,19 @@ def tile_list_road_segment_linking_kernel(
         w2_raw, page, base_rows = {}, {}, {}
         w1_raw = load_fp4_words(w1_words, H, "w1_raw")
         load_scales_side_by_side(w1_plane, w1_scales)
-        tab_sb = [load_table_words(tab_words[0], "tab0")]
         idx = load_list(offs, "idx")
-        tab_sb.append(load_table_words(tab_words[1], "tab1"))
+        tab_sb = [load_table_words(tab_words[0], "tab0")]
         load_scales_side_by_side(tab_plane, tab_scales)
+        tab_sb.append(load_table_words(tab_words[1], "tab1"))
         w2_raw[0, 0] = load_rows(w2, 0, 0, "slab", "w2_raw00")
         w2_raw[1, 0] = load_rows(w2, 1, 0, "slab", "w2_raw10")
-        idx2 = load_list(offs2, "idx2")
-        for q in range(QUADS):
-            nc.sync.dma_start(
-                tab2_plane[32 * q : 32 * q + 8, :].bitcast(I32),
-                tab2_scales[:, 4 * q : 4 * q + 4, :].bitcast(I32),
-            )
-        gain_sb = keep.tile([P, 2, PACK], F32, name="gain_sb")
-        nc.sync.dma_start(gain_sb[:], gain.rearrange("(a p t) -> p a t", a=2, t=PACK))
         idx3 = load_list(offs3, "idx3")
         wgs_sb = keep.tile([P, PACK * S], F32, name="wgs_sb")
         for q in range(QUADS):
             nc.sync.dma_start(wgs_sb[32 * q : 32 * (q + 1), :], wgs.rearrange("(p t) j -> p (t j)", t=PACK))
         page[0, 0] = load_page(0, 0)
+        gain_sb = keep.tile([P, 2, PACK], F32, name="gain_sb")
+        nc.sync.dma_start(gain_sb[:], gain.rearrange("(a p t) -> p a t", a=2, t=PACK))
         page[0, 1] = load_page(0, 1)
         w2_raw[0, 1] = load_rows(w2, 0, 1, "slab", "w2_raw01")
         page[0, 2] = load_page(0, 2)
@@ -113,6 +107,12 @@ def tile_list_road_segment_linking_kernel(
         page[1, 3] = load_page(1, 3)
         for h in range(2):
             base_rows[0, h] = load_rows(base, 0, h, "given", "base0%d" % h)
+        idx2 = load_list(offs2, "idx2")
+        for q in range(QUADS):
+            nc.sync.dma_start(
+                tab2_plane[32 * q : 32 * q + 8, :].bitcast(I32),
+                tab2_scales[:, 4 * q : 4 * q + 4, :].bitcast(I32),
+            )
         tab2_sb = [load_table_words(tab2_words[a], "tab2_%d" % a) for a in range(2)]
         w3_sb = load_fp4_words(w3_words, S2, "w3_sb")
         load_scales_side_by_side(w3_plane, w3_scales)
@@ -155,22 +155,25 @@ def tile_list_road_segment_linking_kernel(
 
         deal_w1(0)
         deal_w1(1)
-        v_plane = [gather(tab_plane[:, T * kp : T * (kp + 1)], idx, U8, "v_plane%d" % kp) for kp in range(2)]
-        v = [gather(tab_sb[kp][:], idx, U32, "v%d" % kp) for kp in range(2)]
-        w2_q = {(0, 0): quantize_w2(0, 0, nc.scalar.copy), (1, 0): quantize_w2(1, 0, nc.vector.tensor_copy)}
-        v2_planes = gather(tab2_plane[:], idx2, U8, "v2_planes")
+        v, v_plane = [], []
+        for kp in range(2):
+            v.append(gather(tab_sb[kp][:], idx, U32, "v%d" % kp))
+            v_plane.append(gather(tab_plane[:, T * kp : T * (kp + 1)], idx, U8, "v_plane%d" % kp))
+        w2_q = {(kp, 0): quantize_w2(kp, 0, nc.vector.tensor_copy) for kp in range(2)}
 
         def bank(i, name):
             return psum.tile([P, BANK], F32, name=name, tag="bank%d" % (i % 8))
 
+        bent_first = ring.tile([P, PACK, S], F32, name="bent_first", tag="slab", bufs=4)
         staged = {
             (a, h): ring.tile([P, PACK, BANK], F32, name="staged%d%d" % (a, h), tag="slab", bufs=4)
-            for a in (1, 0) for h in range(2)
+            for a, h in ((1, 1), (0, 0), (0, 1), (1, 0))
         }
+        bent = {(0, t): bent_first[:, t, :] for t in range(PACK)}
+        bent.update({(1, t): ring.tile([P, S], F32, name="bent", tag="first", bufs=4)[:] for t in range(PACK)})
 
-        def change_page(a, t):
-            x = bank(2 * (PACK * a + t), "x")
-            y = bank(2 * (PACK * a + t) + 1, "y")
+        def bend(a, t):
+            x = bank(t, "x")
             for kp in range(2):
                 col = H * kp + PASS * a + P * t
                 nc.tensor.matmul_mx(
@@ -178,6 +181,10 @@ def tile_list_road_segment_linking_kernel(
                     lhsT_scale=w1_plane_dealt[:, col : col + P],
                     rhs=v[kp][:].bitcast(E4M3), rhs_scale=v_plane[kp][:], start=(kp == 0), stop=(kp == 1),
                 )
+            nc.scalar.activation(bent[a, t], x[:], ACT.Gelu_apprx_tanh)
+
+        def change_page(a, t):
+            y = bank(PACK + t, "y")
             for kp in range(2):
                 codes, plane = w2_q[kp, a]
                 nc.tensor.matmul_mx(
@@ -185,10 +192,8 @@ def tile_list_road_segment_linking_kernel(
                     lhsT_scale=plane[:, P * t : P * (t + 1)],
                     rhs=v[kp][:].bitcast(E4M3), rhs_scale=v_plane[kp][:], start=(kp == 0), stop=(kp == 1),
                 )
-            bent = ring.tile([P, S], F32, name="bent", tag="first")
-            nc.scalar.activation(bent[:], x[:], ACT.Gelu_apprx_tanh)
             feat = ring.tile([P, S], F32, name="feat", tag="second", bufs=3)
-            nc.vector.scalar_tensor_tensor(feat[:], bent[:], gain_sb[:, a, t : t + 1], y[:], ALU.mult, ALU.add)
+            nc.vector.scalar_tensor_tensor(feat[:], bent[a, t], gain_sb[:, a, t : t + 1], y[:], ALU.mult, ALU.add)
             nc.vector.tensor_tensor(
                 page[a, t][:].indirect(idx3[:]), feat[:], wgs_sb[:, S * t : S * (t + 1)], ALU.mult
             )
@@ -215,6 +220,9 @@ def tile_list_road_segment_linking_kernel(
             page_q[a, h] = quantize(page_grouped, "page_%d%d" % (a, h))
             top_q[a, h] = quantize(top_grouped, "top_%d%d" % (a, h))
 
+        for a in range(2):
+            for t in range(PACK):
+                bend(a, t)
         for t in range(PACK - 1):
             change_page(0, t)
         w2_q.update({(kp, 1): quantize_w2(kp, 1, nc.scalar.copy) for kp in range(2)})
@@ -226,6 +234,7 @@ def tile_list_road_segment_linking_kernel(
                 stage_page(a, t)
         for h in range(2):
             quantize_page(0, h)
+        v2_planes = gather(tab2_plane[:], idx2, U8, "v2_planes")
         v2 = [gather(tab2_sb[a][:], idx2, U32, "v2_%d" % a) for a in range(2)]
         minus_road = keep.tile([P, S2 // P], F32, name="minus_road")
         nc.scalar.mul(minus_road[:], road_sb[:], -1.0)
@@ -260,18 +269,21 @@ def tile_list_road_segment_linking_kernel(
             scores[m] = ring.tile([P, T2], F32, name="scores%d" % m, tag="given", bufs=4)
             for h in range(2):
                 nc.scalar.copy(scores[m][:, BANK * h : BANK * (h + 1)], score[m, h][:])
-            picked = ring.tile([P, NP], F32, name="picked", tag="first")
+            picked = ring.tile([P, NP], F32, name="picked", tag="first", bufs=4)
             nc.vector.tensor_copy(picked[:], scores[m][:].indirect(p1[:]))
             shifted[m] = ring.tile([P, NP], F32, name="shifted", tag="second", bufs=3)
             nc.scalar.activation(shifted[m][:], picked[:], ACT.Identity, bias=minus_road[:, m : m + 1])
 
-        def pick_second(m):
-            result = ring.tile([P, NP], F32, name="result")
-            nc.vector.tensor_tensor(result[:], scores[m][:].indirect(p2[:]), shifted[m][:], ALU.mult)
-            nc.sync.dma_start(out[P * m : P * (m + 1), :], result[:])
+        def pick_second(m, parts):
+            width = NP // parts
+            for c in range(0, NP, width):
+                result = ring.tile([P, width], F32, name="result", tag="first", bufs=4)
+                picks = scores[m][:].indirect(p2[:, c // 16 : (c + width) // 16])
+                nc.vector.tensor_tensor(result[:], picks, shifted[m][:, c : c + width], ALU.mult)
+                nc.sync.dma_start(out[P * m : P * (m + 1), c : c + width], result[:])
 
         pick_first(0)
         for m in range(S2 // P):
             if m + 1 < S2 // P:
                 pick_first(m + 1)
-            pick_second(m)
+            pick_second(m, 2 if m + 1 == S2 // P else 1)

@@ -1,6 +1,7 @@
 from contextlib import ExitStack
 
 import concourse.mybir as mybir
+from concourse.masks import make_identity
 
 K, H, T, S, T2, S2, T3, NP = 1024, 1024, 2048, 512, 1024, 512, 2048, 512
 FLOPS = 2 * (2 * K * H * S + 2 * H * S2 * T2)
@@ -44,9 +45,9 @@ def tile_list_road_segment_linking_kernel(
             nc.vector.memset(plane[:].bitcast(I32), 0)
             return plane
 
-        def load_scales_side_by_side(plane, src):
-            for q in range(QUADS):
-                nc.sync.dma_start(
+        def load_scales_side_by_side(plane, src, upper_queue):
+            for q in (0, 2, 1, 3):
+                (nc.sync if q < 2 else upper_queue).dma_start(
                     plane[32 * q : 32 * q + 4, :].bitcast(I32).rearrange("r (a n) -> r a n", a=2),
                     src[:, 4 * q : 4 * q + 4, :].bitcast(I32).rearrange("a r n -> r a n"),
                 )
@@ -82,18 +83,18 @@ def tile_list_road_segment_linking_kernel(
         w3_plane = zeroed_plane(2 * S2, "w3_plane")
 
         w2_raw, page, base_rows = {}, {}, {}
+        wgs_turned = keep.tile([P, S // P, PACK, P], F32, name="wgs_turned")
         w1_raw = load_fp4_words(w1_words, H, "w1_raw")
-        load_scales_side_by_side(w1_plane, w1_scales)
+        load_scales_side_by_side(w1_plane, w1_scales, nc.scalar)
         idx = load_list(offs, "idx")
+        wgs_rows = keep.tile([P, S], F32, name="wgs_rows")
+        nc.sync.dma_start(wgs_rows[:], wgs)
         tab_sb = [load_table_words(tab_words[0], "tab0")]
-        load_scales_side_by_side(tab_plane, tab_scales)
+        load_scales_side_by_side(tab_plane, tab_scales, nc.scalar)
         tab_sb.append(load_table_words(tab_words[1], "tab1"))
         w2_raw[0, 0] = load_rows(w2, 0, 0, "slab", "w2_raw00")
         w2_raw[1, 0] = load_rows(w2, 1, 0, "slab", "w2_raw10")
         idx3 = load_list(offs3, "idx3")
-        wgs_sb = keep.tile([P, PACK * S], F32, name="wgs_sb")
-        for q in range(QUADS):
-            nc.sync.dma_start(wgs_sb[32 * q : 32 * (q + 1), :], wgs.rearrange("(p t) j -> p (t j)", t=PACK))
         page[0, 0] = load_page(0, 0)
         gain_sb = keep.tile([P, 2, PACK], F32, name="gain_sb")
         nc.sync.dma_start(gain_sb[:], gain.rearrange("(a p t) -> p a t", a=2, t=PACK))
@@ -115,7 +116,7 @@ def tile_list_road_segment_linking_kernel(
             )
         tab2_sb = [load_table_words(tab2_words[a], "tab2_%d" % a) for a in range(2)]
         w3_sb = load_fp4_words(w3_words, S2, "w3_sb")
-        load_scales_side_by_side(w3_plane, w3_scales)
+        load_scales_side_by_side(w3_plane, w3_scales, nc.sync)
         for h in range(2):
             base_rows[1, h] = load_rows(base, 1, h, "given", "base1%d" % h)
         p1 = load_list(pos1, "p1")
@@ -159,10 +160,27 @@ def tile_list_road_segment_linking_kernel(
         for kp in range(2):
             v.append(gather(tab_sb[kp][:], idx, U32, "v%d" % kp))
             v_plane.append(gather(tab_plane[:, T * kp : T * (kp + 1)], idx, U8, "v_plane%d" % kp))
-        w2_q = {(kp, 0): quantize_w2(kp, 0, nc.vector.tensor_copy) for kp in range(2)}
 
         def bank(i, name):
-            return psum.tile([P, BANK], F32, name=name, tag="bank%d" % (i % 8))
+            return psum.tile([P, BANK], F32, name=name, tag="bank%d" % i)
+
+        identity = keep.tile([P, P], F32, name="identity")
+        make_identity(nc, identity[:])
+        turned = bank(PACK, "turned")
+        for b in range(S // P):
+            nc.tensor.transpose(turned[:, P * b : P * (b + 1)], wgs_rows[:, P * b : P * (b + 1)], identity[:])
+        nc.scalar.copy(
+            wgs_turned[:].rearrange("p b t (q s) -> p b t q s", q=QUADS),
+            turned[:].rearrange("p (b s t) -> p b t s", t=PACK, s=32).unsqueeze(3).to_broadcast([P, S // P, PACK, QUADS, 32]),
+        )
+        wgs_sb = keep.tile([P, PACK * S], F32, name="wgs_sb")
+        for t in range(PACK):
+            dealt = bank(t, "dealt")
+            for b in range(S // P):
+                nc.tensor.transpose(dealt[:, P * b : P * (b + 1)], wgs_turned[:, b, t, :], identity[:])
+            nc.scalar.copy(wgs_sb[:, S * t : S * (t + 1)], dealt[:])
+
+        w2_q = {(kp, 0): quantize_w2(kp, 0, nc.vector.tensor_copy) for kp in range(2)}
 
         bent_first = ring.tile([P, PACK, S], F32, name="bent_first", tag="slab", bufs=4)
         staged = {
@@ -183,7 +201,9 @@ def tile_list_road_segment_linking_kernel(
                 )
             nc.scalar.activation(bent[a, t], x[:], ACT.Gelu_apprx_tanh)
 
-        def change_page(a, t):
+        feats = {}
+
+        def make_features(a, t):
             y = bank(PACK + t, "y")
             for kp in range(2):
                 codes, plane = w2_q[kp, a]
@@ -194,8 +214,11 @@ def tile_list_road_segment_linking_kernel(
                 )
             feat = ring.tile([P, S], F32, name="feat", tag="second", bufs=3)
             nc.vector.scalar_tensor_tensor(feat[:], bent[a, t], gain_sb[:, a, t : t + 1], y[:], ALU.mult, ALU.add)
+            feats[a, t] = feat
+
+        def change_page(a, t):
             nc.vector.tensor_tensor(
-                page[a, t][:].indirect(idx3[:]), feat[:], wgs_sb[:, S * t : S * (t + 1)], ALU.mult
+                page[a, t][:].indirect(idx3[:]), feats[a, t][:], wgs_sb[:, S * t : S * (t + 1)], ALU.mult
             )
 
         def stage_page(a, t):
@@ -223,12 +246,14 @@ def tile_list_road_segment_linking_kernel(
         for a in range(2):
             for t in range(PACK):
                 bend(a, t)
-        for t in range(PACK - 1):
-            change_page(0, t)
-        w2_q.update({(kp, 1): quantize_w2(kp, 1, nc.scalar.copy) for kp in range(2)})
-        change_page(0, PACK - 1)
-        for t in range(PACK):
-            change_page(1, t)
+        tiles = [(a, t) for a in range(2) for t in range(PACK)]
+        make_features(*tiles[0])
+        for here, ahead in zip(tiles, tiles[1:] + [None]):
+            if ahead == (1, 0):
+                w2_q.update({(kp, 1): quantize_w2(kp, 1, nc.scalar.copy) for kp in range(2)})
+            if ahead is not None:
+                make_features(*ahead)
+            change_page(*here)
         for a in range(2):
             for t in range(PACK):
                 stage_page(a, t)

@@ -65,10 +65,12 @@ def tile_list_road_segment_linking_kernel(
             )
             return words
 
-        def load_rows(src, a, h, tag, name):
-            dst = ring.tile([P, PACK, BANK], F32, name=name, tag=tag, bufs=4)
-            rows = src[PASS * a : PASS * (a + 1), BANK * h : BANK * (h + 1)]
-            nc.sync.dma_start(dst[:], rows.rearrange("(p i) c -> p i c", i=PACK))
+        def load_rows(src, a, h, tag, bufs, name, parts=1):
+            dst = ring.tile([P, PACK, BANK], F32, name=name, tag=tag, bufs=bufs, align_bytes=64)
+            rows = src[PASS * a : PASS * (a + 1), BANK * h : BANK * (h + 1)].rearrange("(p i) c -> p i c", i=PACK)
+            width = BANK // parts
+            for c in range(0, BANK, width):
+                nc.sync.dma_start(dst[:, :, c : c + width], rows[:, :, c : c + width])
             return dst
 
         def load_page(a, t):
@@ -92,22 +94,22 @@ def tile_list_road_segment_linking_kernel(
         tab_sb = [load_table_words(tab_words[0], "tab0")]
         load_scales_side_by_side(tab_plane, tab_scales, nc.scalar)
         tab_sb.append(load_table_words(tab_words[1], "tab1"))
-        w2_raw[0, 0] = load_rows(w2, 0, 0, "slab", "w2_raw00")
-        w2_raw[1, 0] = load_rows(w2, 1, 0, "slab", "w2_raw10")
+        w2_raw[0, 0] = load_rows(w2, 0, 0, "slab", 4, "w2_raw00")
+        w2_raw[1, 0] = load_rows(w2, 1, 0, "slab", 4, "w2_raw10")
         idx3 = load_list(offs3, "idx3")
         page[0, 0] = load_page(0, 0)
         gain_sb = keep.tile([P, 2, PACK], F32, name="gain_sb")
         nc.sync.dma_start(gain_sb[:], gain.rearrange("(a p t) -> p a t", a=2, t=PACK))
         page[0, 1] = load_page(0, 1)
-        w2_raw[0, 1] = load_rows(w2, 0, 1, "slab", "w2_raw01")
+        w2_raw[0, 1] = load_rows(w2, 0, 1, "slab", 4, "w2_raw01")
         page[0, 2] = load_page(0, 2)
-        w2_raw[1, 1] = load_rows(w2, 1, 1, "slab", "w2_raw11")
+        w2_raw[1, 1] = load_rows(w2, 1, 1, "slab", 4, "w2_raw11")
         for t in range(PACK - 1):
             page[1, t] = load_page(1, t)
         page[0, 3] = load_page(0, 3)
         page[1, 3] = load_page(1, 3)
         for h in range(2):
-            base_rows[0, h] = load_rows(base, 0, h, "given", "base0%d" % h)
+            base_rows[0, h] = load_rows(base, 0, h, "given", 3, "base0%d" % h)
         idx2 = load_list(offs2, "idx2")
         for q in range(QUADS):
             nc.sync.dma_start(
@@ -117,8 +119,8 @@ def tile_list_road_segment_linking_kernel(
         tab2_sb = [load_table_words(tab2_words[a], "tab2_%d" % a) for a in range(2)]
         w3_sb = load_fp4_words(w3_words, S2, "w3_sb")
         load_scales_side_by_side(w3_plane, w3_scales, nc.sync)
-        for h in range(2):
-            base_rows[1, h] = load_rows(base, 1, h, "given", "base1%d" % h)
+        base_rows[1, 0] = load_rows(base, 1, 0, "given", 3, "base10")
+        base_rows[1, 1] = load_rows(base, 1, 1, "last", 1, "base11")
         p1 = load_list(pos1, "p1")
         p2 = load_list(pos2, "p2")
         road_sb = keep.tile([P, S2 // P], F32, name="road_sb")
@@ -130,32 +132,32 @@ def tile_list_road_segment_linking_kernel(
             nc.vector.tensor_copy(dst[:], window.indirect(offsets[:]))
             return dst
 
-        def quantize(grouped, name):
+        def quantize(grouped, name, cuts=(0, BANK)):
             codes = keep.tile([P, BANK], U32, name=name + "_codes", align_bytes=64)
             plane = keep.tile([P, BANK], U8, name=name + "_plane", align_bytes=64)
-            nc.vector.quantize_mx(out=codes[:].bitcast(E4M3), scales=plane[:], in_=grouped[:])
+            for lo, hi in zip(cuts, cuts[1:]):
+                nc.vector.quantize_mx(
+                    out=codes[:, lo:hi].bitcast(E4M3), scales=plane[:, lo:hi], in_=grouped[:, PACK * lo : PACK * hi]
+                )
             return codes, plane
 
-        def quantize_w2(kp, a, copy):
+        def quantize_w2(kp, a, copy, parts=1, cuts=(0, BANK)):
             grouped = ring.tile([P, PACK * BANK], BF16, name="w2_grouped", tag="grouped", align_bytes=64)
-            copy(
-                grouped[:].rearrange("p (t m i) -> p m i t", t=PACK, i=PACK),
-                w2_raw[kp, a][:].rearrange("p i (m t) -> p m i t", t=PACK),
-            )
-            return quantize(grouped, "w2_%d%d" % (kp, a))
+            width = P // parts
+            for m in range(0, P, width):
+                copy(
+                    grouped[:].rearrange("p (t m i) -> p m i t", t=PACK, i=PACK)[:, m : m + width],
+                    w2_raw[kp, a][:].rearrange("p i (m t) -> p m i t", t=PACK)[:, m : m + width],
+                )
+            return quantize(grouped, "w2_%d%d" % (kp, a), cuts)
 
         w1_dealt = keep.tile([P, 2 * 2 * H], U8, name="w1_dealt", align_bytes=64)
         w1_plane_dealt = keep.tile([P, 2 * H], U8, name="w1_plane_dealt", align_bytes=64)
 
-        def deal_w1(a):
-            for dst, src in ((w1_dealt[:].bitcast(U16), w1_raw[:].bitcast(U16)), (w1_plane_dealt[:], w1_plane[:])):
-                nc.vector.tensor_copy(
-                    dst.rearrange("p (k a t m) -> p a k m t", k=2, a=2, t=PACK)[:, a],
-                    src.rearrange("p (k a m t) -> p a k m t", k=2, a=2, t=PACK)[:, a],
-                )
-
-        deal_w1(0)
-        deal_w1(1)
+        for dst, src in ((w1_dealt[:].bitcast(U16), w1_raw[:].bitcast(U16)), (w1_plane_dealt[:], w1_plane[:])):
+            nc.vector.tensor_copy(
+                dst.rearrange("p (g t m) -> p g m t", g=4, t=PACK), src.rearrange("p (g m t) -> p g m t", g=4, t=PACK)
+            )
         v, v_plane = [], []
         for kp in range(2):
             v.append(gather(tab_sb[kp][:], idx, U32, "v%d" % kp))
@@ -180,11 +182,14 @@ def tile_list_road_segment_linking_kernel(
                 nc.tensor.transpose(dealt[:, P * b : P * (b + 1)], wgs_turned[:, b, t, :], identity[:])
             nc.scalar.copy(wgs_sb[:, S * t : S * (t + 1)], dealt[:])
 
-        w2_q = {(kp, 0): quantize_w2(kp, 0, nc.vector.tensor_copy) for kp in range(2)}
+        w2_q = {
+            (0, 0): quantize_w2(0, 0, nc.vector.tensor_copy),
+            (1, 0): quantize_w2(1, 0, nc.vector.tensor_copy, cuts=(0, P, BANK)),
+        }
 
-        bent_first = ring.tile([P, PACK, S], F32, name="bent_first", tag="slab", bufs=4)
+        bent_first = ring.tile([P, PACK, S], F32, name="bent_first", tag="slab", bufs=4, align_bytes=64)
         staged = {
-            (a, h): ring.tile([P, PACK, BANK], F32, name="staged%d%d" % (a, h), tag="slab", bufs=4)
+            (a, h): ring.tile([P, PACK, BANK], F32, name="staged%d%d" % (a, h), tag="slab", bufs=4, align_bytes=64)
             for a, h in ((1, 1), (0, 0), (0, 1), (1, 0))
         }
         bent = {(0, t): bent_first[:, t, :] for t in range(PACK)}
@@ -260,38 +265,56 @@ def tile_list_road_segment_linking_kernel(
         for h in range(2):
             quantize_page(0, h)
         v2_planes = gather(tab2_plane[:], idx2, U8, "v2_planes")
-        v2 = [gather(tab2_sb[a][:], idx2, U32, "v2_%d" % a) for a in range(2)]
+        half = S2 // 2
+        v2_first = keep.tile([P, 2, half], U32, name="v2_first", align_bytes=64)
+        for a in range(2):
+            nc.vector.tensor_copy(v2_first[:, a, :], tab2_sb[a][:].indirect(idx2[:, : half // 16]))
         minus_road = keep.tile([P, S2 // P], F32, name="minus_road")
         nc.scalar.mul(minus_road[:], road_sb[:], -1.0)
 
         score = {(m, h): bank(2 * m + h, "score%d%d" % (m, h)) for m in range(S2 // P) for h in range(2)}
 
-        def score_passes(a, h):
-            for m in range(S2 // P):
-                codes, plane = page_q[a, h]
-                nc.tensor.matmul_mx(
-                    out=score[m, h][:], lhsT=v2[a][:, P * m : P * (m + 1)].bitcast(E4M3),
-                    lhsT_scale=v2_planes[4 * a :, P * m : P * (m + 1)],
-                    rhs=codes[:].bitcast(E4M3), rhs_scale=plane[:], start=(a == 0), stop=False,
-                )
-                codes, plane = top_q[a, h]
-                col = S2 * a + P * m
-                nc.tensor.matmul_mx(
-                    out=score[m, h][:], lhsT=w3_sb[:, 2 * col : 2 * (col + P)].bitcast(E2M1),
-                    lhsT_scale=w3_plane[:, col : col + P],
-                    rhs=codes[:].bitcast(E4M3), rhs_scale=plane[:], start=False, stop=(a == 1),
-                )
+        def page_pass(m, a, h, v2, start, stop):
+            codes, plane = page_q[a, h]
+            nc.tensor.matmul_mx(
+                out=score[m, h][:], lhsT=v2[:, a, P * (m % 2) : P * (m % 2 + 1)].bitcast(E4M3),
+                lhsT_scale=v2_planes[4 * a :, P * m : P * (m + 1)],
+                rhs=codes[:].bitcast(E4M3), rhs_scale=plane[:], start=start, stop=stop,
+            )
+
+        def top_pass(m, a, h, start, stop):
+            codes, plane = top_q[a, h]
+            col = S2 * a + P * m
+            nc.tensor.matmul_mx(
+                out=score[m, h][:], lhsT=w3_sb[:, 2 * col : 2 * (col + P)].bitcast(E2M1),
+                lhsT_scale=w3_plane[:, col : col + P],
+                rhs=codes[:].bitcast(E4M3), rhs_scale=plane[:], start=start, stop=stop,
+            )
+
+        def early_passes(a, h):
+            for m in (0, 1):
+                page_pass(m, a, h, v2_first, a == 0, False)
+                top_pass(m, a, h, False, a == 1)
+            for m in (2, 3):
+                top_pass(m, a, h, a == 0, False)
 
         for h in range(2):
-            score_passes(0, h)
+            early_passes(0, h)
         for h in range(2):
             quantize_page(1, h)
-            score_passes(1, h)
+            early_passes(1, h)
+        v2_last = ring.tile([P, 2, half], U32, name="v2_last", tag="last", bufs=1, align_bytes=64)
+        for a in range(2):
+            nc.vector.tensor_copy(v2_last[:, a, :], tab2_sb[a][:].indirect(idx2[:, half // 16 :]))
+        for m in (2, 3):
+            for h in range(2):
+                for a in range(2):
+                    page_pass(m, a, h, v2_last, False, a == 1)
 
         scores, shifted = {}, {}
 
         def pick_first(m):
-            scores[m] = ring.tile([P, T2], F32, name="scores%d" % m, tag="given", bufs=4)
+            scores[m] = ring.tile([P, T2], F32, name="scores%d" % m, tag="given", bufs=3, align_bytes=64)
             for h in range(2):
                 nc.scalar.copy(scores[m][:, BANK * h : BANK * (h + 1)], score[m, h][:])
             picked = ring.tile([P, NP], F32, name="picked", tag="first", bufs=4)

from contextlib import ExitStack

import concourse.mybir as mybir
from concourse.masks import make_identity

K, H, T, S, T2, S2, T3, NP = 1024, 1024, 2048, 512, 1024, 512, 2048, 512
FLOPS = 2 * (2 * K * H * S + 2 * H * S2 * T2)

F32 = mybir.dt.float32
BF16 = mybir.dt.bfloat16
I32 = mybir.dt.int32
U32 = mybir.dt.uint32
U16 = mybir.dt.uint16
U8 = mybir.dt.uint8
E4M3 = mybir.dt.float8_e4m3fn_x4
E2M1 = mybir.dt.float4_e2m1fn_x4
ALU = mybir.AluOpType
ACT = mybir.ActivationFunctionType

P = 128
PACK = 4
PASS = P * PACK
BANK = 512
QUADS = 4


def tile_list_road_segment_linking_kernel(
    tc, tab_words, tab_scales, offs, tab2_words, tab2_scales, offs2, offs3, pos1, pos2,
    w1_words, w1_scales, w3_words, w3_scales, w2, gain, wgs, page0, base, road, out,
):
    nc = tc.nc
    with ExitStack() as ctx:
        lists = ctx.enter_context(tc.tile_pool(name="lists", bufs=1))
        keep = ctx.enter_context(tc.tile_pool(name="keep", bufs=1))
        ring = ctx.enter_context(tc.tile_pool(name="ring", bufs=2))
        psum = ctx.enter_context(tc.psum_pool(name="psum", bufs=1))

        def load_list(src, name):
            dst = lists.tile([P, S // 16], U16, name=name)
            nc.sync.dma_start(dst[:], src)
            return dst

        def zeroed_plane(width, name):
            plane = keep.tile([P, width], U8, name=name, align_bytes=64)
            nc.vector.memset(plane[:].bitcast(I32), 0)
            return plane

        def load_scales_side_by_side(plane, src, upper_queue):
            for q in (0, 2, 1, 3):
                (nc.sync if q < 2 else upper_queue).dma_start(
                    plane[32 * q : 32 * q + 4, :].bitcast(I32).rearrange("r (a n) -> r a n", a=2),
                    src[:, 4 * q : 4 * q + 4, :].bitcast(I32).rearrange("a r n -> r a n"),
                )

        def load_table_words(src, name):
            words = keep.tile([P, T], U32, name=name, align_bytes=64)
            nc.sync.dma_start(words[:].bitcast(I32), src.rearrange("p n i -> p (n i)").bitcast(I32))
            return words

        def load_fp4_words(src, cols, name):
            words = keep.tile([P, 2 * 2 * cols], U8, name=name, align_bytes=64)
            nc.sync.dma_start(
                words[:].bitcast(I32).rearrange("p (a n) -> p a n", a=2),
                src.bitcast(I32).rearrange("a p n -> p a n"),
            )
            return words

        def load_rows(src, a, h, tag, bufs, name, parts=1):
            dst = ring.tile([P, PACK, BANK], F32, name=name, tag=tag, bufs=bufs, align_bytes=64)
            rows = src[PASS * a : PASS * (a + 1), BANK * h : BANK * (h + 1)].rearrange("(p i) c -> p i c", i=PACK)
            width = BANK // parts
            for c in range(0, BANK, width):
                nc.sync.dma_start(dst[:, :, c : c + width], rows[:, :, c : c + width])
            return dst

        def load_page(a, t):
            dst = keep.tile([P, T2], F32, name="page%d%d" % (a, t))
            rows = page0[PASS * a : PASS * (a + 1), :].rearrange("(p i) n -> p i n", i=PACK)
            nc.sync.dma_start(dst[:], rows[:, t, :])
            return dst

        w1_plane = zeroed_plane(2 * H, "w1_plane")
        tab_plane = zeroed_plane(2 * T, "tab_plane")
        tab2_plane = zeroed_plane(T3, "tab2_plane")
        w3_plane = zeroed_plane(2 * S2, "w3_plane")

        w2_raw, page, base_rows = {}, {}, {}
        wgs_turned = keep.tile([P, S // P, PACK, P], F32, name="wgs_turned")
        w1_raw = load_fp4_words(w1_words, H, "w1_raw")
        load_scales_side_by_side(w1_plane, w1_scales, nc.scalar)
        idx = load_list(offs, "idx")
        wgs_rows = keep.tile([P, S], F32, name="wgs_rows")
        nc.sync.dma_start(wgs_rows[:], wgs)
        tab_sb = [load_table_words(tab_words[0], "tab0")]
        load_scales_side_by_side(tab_plane, tab_scales, nc.scalar)
        tab_sb.append(load_table_words(tab_words[1], "tab1"))
        w2_raw[0, 0] = load_rows(w2, 0, 0, "slab", 4, "w2_raw00")
        w2_raw[1, 0] = load_rows(w2, 1, 0, "slab", 4, "w2_raw10")
        idx3 = load_list(offs3, "idx3")
        page[0, 0] = load_page(0, 0)
        gain_sb = keep.tile([P, 2, PACK], F32, name="gain_sb")
        nc.sync.dma_start(gain_sb[:], gain.rearrange("(a p t) -> p a t", a=2, t=PACK))
        page[0, 1] = load_page(0, 1)
        w2_raw[0, 1] = load_rows(w2, 0, 1, "slab", 4, "w2_raw01")
        page[0, 2] = load_page(0, 2)
        w2_raw[1, 1] = load_rows(w2, 1, 1, "slab", 4, "w2_raw11")
        for t in range(PACK - 1):
            page[1, t] = load_page(1, t)
        page[0, 3] = load_page(0, 3)
        page[1, 3] = load_page(1, 3)
        for h in range(2):
            base_rows[0, h] = load_rows(base, 0, h, "given", 3, "base0%d" % h)
        idx2 = load_list(offs2, "idx2")
        for q in range(QUADS):
            nc.sync.dma_start(
                tab2_plane[32 * q : 32 * q + 8, :].bitcast(I32),
                tab2_scales[:, 4 * q : 4 * q + 4, :].bitcast(I32),
            )
        tab2_sb = [load_table_words(tab2_words[a], "tab2_%d" % a) for a in range(2)]
        w3_sb = load_fp4_words(w3_words, S2, "w3_sb")
        load_scales_side_by_side(w3_plane, w3_scales, nc.sync)
        base_rows[1, 0] = load_rows(base, 1, 0, "given", 3, "base10")
        base_rows[1, 1] = load_rows(base, 1, 1, "last", 1, "base11")
        p1 = load_list(pos1, "p1")
        p2 = load_list(pos2, "p2")
        road_sb = keep.tile([P, S2 // P], F32, name="road_sb")
        with nc.allow_non_contiguous_dma(reason="one value of road a partition and row tile"):
            nc.sync.dma_start(road_sb[:], road.rearrange("(m p) -> p m", p=P))

        def gather(window, offsets, dtype, name):
            dst = keep.tile([P, S], dtype, name=name, align_bytes=64)
            nc.vector.tensor_copy(dst[:], window.indirect(offsets[:]))
            return dst

        def quantize(grouped, name, cuts=(0, BANK)):
            codes = keep.tile([P, BANK], U32, name=name + "_codes", align_bytes=64)
            plane = keep.tile([P, BANK], U8, name=name + "_plane", align_bytes=64)
            for lo, hi in zip(cuts, cuts[1:]):
                nc.vector.quantize_mx(
                    out=codes[:, lo:hi].bitcast(E4M3), scales=plane[:, lo:hi], in_=grouped[:, PACK * lo : PACK * hi]
                )
            return codes, plane

        def quantize_w2(kp, a, copy, parts=1, cuts=(0, BANK)):
            grouped = ring.tile([P, PACK * BANK], BF16, name="w2_grouped", tag="grouped", align_bytes=64)
            width = P // parts
            for m in range(0, P, width):
                copy(
                    grouped[:].rearrange("p (t m i) -> p m i t", t=PACK, i=PACK)[:, m : m + width],
                    w2_raw[kp, a][:].rearrange("p i (m t) -> p m i t", t=PACK)[:, m : m + width],
                )
            return quantize(grouped, "w2_%d%d" % (kp, a), cuts)

        w1_dealt = keep.tile([P, 2 * 2 * H], U8, name="w1_dealt", align_bytes=64)
        w1_plane_dealt = keep.tile([P, 2 * H], U8, name="w1_plane_dealt", align_bytes=64)

        for dst, src in ((w1_dealt[:].bitcast(U16), w1_raw[:].bitcast(U16)), (w1_plane_dealt[:], w1_plane[:])):
            nc.vector.tensor_copy(
                dst.rearrange("p (g t m) -> p g m t", g=4, t=PACK), src.rearrange("p (g m t) -> p g m t", g=4, t=PACK)
            )
        v, v_plane = [], []
        for kp in range(2):
            v.append(gather(tab_sb[kp][:], idx, U32, "v%d" % kp))
            v_plane.append(gather(tab_plane[:, T * kp : T * (kp + 1)], idx, U8, "v_plane%d" % kp))

        def bank(i, name):
            return psum.tile([P, BANK], F32, name=name, tag="bank%d" % i)

        identity = keep.tile([P, P], F32, name="identity")
        make_identity(nc, identity[:])
        turned = bank(PACK, "turned")
        for b in range(S // P):
            nc.tensor.transpose(turned[:, P * b : P * (b + 1)], wgs_rows[:, P * b : P * (b + 1)], identity[:])
        nc.scalar.copy(
            wgs_turned[:].rearrange("p b t (q s) -> p b t q s", q=QUADS),
            turned[:].rearrange("p (b s t) -> p b t s", t=PACK, s=32).unsqueeze(3).to_broadcast([P, S // P, PACK, QUADS, 32]),
        )
        wgs_sb = keep.tile([P, PACK * S], F32, name="wgs_sb")
        for t in range(PACK):
            dealt = bank(t, "dealt")
            for b in range(S // P):
                nc.tensor.transpose(dealt[:, P * b : P * (b + 1)], wgs_turned[:, b, t, :], identity[:])
            nc.scalar.copy(wgs_sb[:, S * t : S * (t + 1)], dealt[:])

        w2_q = {
            (0, 0): quantize_w2(0, 0, nc.vector.tensor_copy),
            (1, 0): quantize_w2(1, 0, nc.vector.tensor_copy, cuts=(0, P, BANK)),
        }

        bent_first = ring.tile([P, PACK, S], F32, name="bent_first", tag="slab", bufs=4, align_bytes=64)
        staged = {
            (a, h): ring.tile([P, PACK, BANK], F32, name="staged%d%d" % (a, h), tag="slab", bufs=4, align_bytes=64)
            for a, h in ((1, 1), (0, 0), (0, 1), (1, 0))
        }
        bent = {(0, t): bent_first[:, t, :] for t in range(PACK)}
        bent.update({(1, t): ring.tile([P, S], F32, name="bent", tag="first", bufs=4)[:] for t in range(PACK)})

        def bend(a, t):
            x = bank(t, "x")
            for kp in range(2):
                col = H * kp + PASS * a + P * t
                nc.tensor.matmul_mx(
                    out=x[:], lhsT=w1_dealt[:, 2 * col : 2 * (col + P)].bitcast(E2M1),
                    lhsT_scale=w1_plane_dealt[:, col : col + P],
                    rhs=v[kp][:].bitcast(E4M3), rhs_scale=v_plane[kp][:], start=(kp == 0), stop=(kp == 1),
                )
            nc.scalar.activation(bent[a, t], x[:], ACT.Gelu_apprx_tanh)

        feats = {}

        def make_features(a, t):
            y = bank(PACK + t, "y")
            for kp in range(2):
                codes, plane = w2_q[kp, a]
                nc.tensor.matmul_mx(
                    out=y[:], lhsT=codes[:, P * t : P * (t + 1)].bitcast(E4M3),
                    lhsT_scale=plane[:, P * t : P * (t + 1)],
                    rhs=v[kp][:].bitcast(E4M3), rhs_scale=v_plane[kp][:], start=(kp == 0), stop=(kp == 1),
                )
            feat = ring.tile([P, S], F32, name="feat", tag="second", bufs=3)
            nc.vector.scalar_tensor_tensor(feat[:], bent[a, t], gain_sb[:, a, t : t + 1], y[:], ALU.mult, ALU.add)
            feats[a, t] = feat

        def change_page(a, t):
            nc.vector.tensor_tensor(
                page[a, t][:].indirect(idx3[:]), feats[a, t][:], wgs_sb[:, S * t : S * (t + 1)], ALU.mult
            )

        def stage_page(a, t):
            for h in range(2):
                nc.scalar.copy(staged[a, h][:, t, :], page[a, t][:, BANK * h : BANK * (h + 1)])

        def by_lines(rows):
            return rows[:].rearrange("p t (c i) -> p c t i", i=4)

        def grouped_by_lines(grouped):
            return grouped[:].rearrange("p (c i t) -> p c t i", i=4, t=PACK)

        page_q, top_q = {}, {}

        def quantize_page(a, h):
            page_grouped = ring.tile([P, PACK * BANK], BF16, name="page_grouped", tag="grouped", align_bytes=64)
            nc.scalar.copy(grouped_by_lines(page_grouped), by_lines(staged[a, h]))
            top_grouped = ring.tile([P, PACK * BANK], BF16, name="top_grouped", align_bytes=64)
            nc.vector.tensor_tensor(
                grouped_by_lines(top_grouped), by_lines(staged[a, h]), by_lines(base_rows[a, h]), ALU.max
            )
            page_q[a, h] = quantize(page_grouped, "page_%d%d" % (a, h))
            top_q[a, h] = quantize(top_grouped, "top_%d%d" % (a, h))

        for a in range(2):
            for t in range(PACK):
                bend(a, t)
        tiles = [(a, t) for a in range(2) for t in range(PACK)]
        make_features(*tiles[0])
        for here, ahead in zip(tiles, tiles[1:] + [None]):
            if ahead == (1, 0):
                w2_q.update({(kp, 1): quantize_w2(kp, 1, nc.scalar.copy) for kp in range(2)})
            if ahead is not None:
                make_features(*ahead)
            change_page(*here)
        for a in range(2):
            for t in range(PACK):
                stage_page(a, t)
        for h in range(2):
            quantize_page(0, h)
        v2_planes = gather(tab2_plane[:], idx2, U8, "v2_planes")
        half = S2 // 2
        v2_first = keep.tile([P, 2, half], U32, name="v2_first", align_bytes=64)
        for a in range(2):
            nc.vector.tensor_copy(v2_first[:, a, :], tab2_sb[a][:].indirect(idx2[:, : half // 16]))
        minus_road = keep.tile([P, S2 // P], F32, name="minus_road")
        nc.scalar.mul(minus_road[:], road_sb[:], -1.0)

        score = {(m, h): bank(2 * m + h, "score%d%d" % (m, h)) for m in range(S2 // P) for h in range(2)}

        def page_pass(m, a, h, v2, start, stop):
            codes, plane = page_q[a, h]
            nc.tensor.matmul_mx(
                out=score[m, h][:], lhsT=v2[:, a, P * (m % 2) : P * (m % 2 + 1)].bitcast(E4M3),
                lhsT_scale=v2_planes[4 * a :, P * m : P * (m + 1)],
                rhs=codes[:].bitcast(E4M3), rhs_scale=plane[:], start=start, stop=stop,
            )

        def top_pass(m, a, h, start, stop):
            codes, plane = top_q[a, h]
            col = S2 * a + P * m
            nc.tensor.matmul_mx(
                out=score[m, h][:], lhsT=w3_sb[:, 2 * col : 2 * (col + P)].bitcast(E2M1),
                lhsT_scale=w3_plane[:, col : col + P],
                rhs=codes[:].bitcast(E4M3), rhs_scale=plane[:], start=start, stop=stop,
            )

        def early_passes(a, h):
            for m in (0, 1):
                page_pass(m, a, h, v2_first, a == 0, False)
                top_pass(m, a, h, False, a == 1)
            for m in (2, 3):
                top_pass(m, a, h, a == 0, False)

        for h in range(2):
            early_passes(0, h)
        for h in range(2):
            quantize_page(1, h)
            early_passes(1, h)
        v2_last = ring.tile([P, 2, half], U32, name="v2_last", tag="last", bufs=1, align_bytes=64)
        for a in range(2):
            nc.vector.tensor_copy(v2_last[:, a, :], tab2_sb[a][:].indirect(idx2[:, half // 16 :]))
        for m in (2, 3):
            for h in range(2):
                for a in range(2):
                    page_pass(m, a, h, v2_last, False, a == 1)

        scores, shifted = {}, {}

        def pick_first(m):
            scores[m] = ring.tile([P, T2], F32, name="scores%d" % m, tag="given", bufs=3, align_bytes=64)
            for h in range(2):
                nc.scalar.copy(scores[m][:, BANK * h : BANK * (h + 1)], score[m, h][:])
            picked = ring.tile([P, NP], F32, name="picked", tag="first", bufs=4)
            nc.vector.tensor_copy(picked[:], scores[m][:].indirect(p1[:]))
            shifted[m] = ring.tile([P, NP], F32, name="shifted", tag="second", bufs=3)
            nc.scalar.activation(shifted[m][:], picked[:], ACT.Identity, bias=minus_road[:, m : m + 1])

        def pick_second(m, parts):
            width = NP // parts
            for c in range(0, NP, width):
                result = ring.tile([P, width], F32, name="result", tag="first", bufs=4)
                picks = scores[m][:].indirect(p2[:, c // 16 : (c + width) // 16])
                nc.vector.tensor_tensor(result[:], picks, shifted[m][:, c : c + width], ALU.mult)
                nc.sync.dma_start(out[P * m : P * (m + 1), c : c + width], result[:])

        pick_first(0)
        for m in range(S2 // P):
            if m + 1 < S2 // P:
                pick_first(m + 1)
            pick_second(m, 2 if m + 1 == S2 // P else 1)
